import numpy as np, ml_dtypes
CORES = [40,64,80,88,96,104,120,144]
N = 8
import mx_ref
BF = ml_dtypes.bfloat16
def entries(a):
    return np.ascontiguousarray(a.T).reshape(-1)
def table(e):
    return np.ascontiguousarray(np.reshape(e, (-1, 16)).T).astype(np.int32)
def cols(t, e):
    v = np.concatenate([t.reshape(128, -1, 4), np.zeros((128, 1, 4), BF)], axis=1)
    return np.ascontiguousarray(v[:, e]).reshape(128, -1)
def f(rng, *shape):
    return mx_ref.flush((rng.standard_normal(shape, dtype=np.float32) * np.exp2(rng.integers(-2, 3, shape[:-1] + (1,)))).astype(BF))
def wide(rng, *shape, cols=0):
    v = rng.standard_normal(shape, dtype=np.float32) * np.exp2(rng.integers(-12, 13, shape)).astype(np.float32)
    if cols: v *= np.repeat(np.exp2(rng.integers(-cols, cols + 1, shape[:-2] + (1, shape[-1] // 4))) * (rng.random(shape[:-2] + (1, shape[-1] // 4)) > 0.0625), 4, axis=-1).astype(np.float32)
    return mx_ref.flush(v.astype(BF))
T, CAPP = 256, 48
def even(n):
    return [T // n + (k < T % n) for k in range(n)]
def counts(rng, h, moves=10 * N * N):
    n = np.array([[h[(d - s) % N] for d in range(N)] for s in range(N)])[rng.permutation(N)][:, rng.permutation(N)]
    top = np.where(n > 0, CAPP, 0)
    for _ in range(moves):
        a, b = rng.permutation(N)[:2]; c, e = rng.permutation(N)[:2]
        k = rng.integers(0, min(n[a, e], n[b, c], top[a, c] - n[a, c], top[b, e] - n[b, e]) + 1)
        n[a, c] += k; n[b, e] += k; n[a, e] -= k; n[b, c] -= k
    return n
def lists(rng, n, back=False):
    a = np.full((N, N, CAPP), -1)
    for s in range(N):
        p = np.arange(T)[::-1] if back else rng.permutation(T)
        for d in range(N):
            k = rng.permutation(CAPP)[:n[s, d]]
            if back: k = np.sort(k)
            a[s, d, k] = p[:n[s, d]]; p = p[n[s, d]:]
    m = []
    for d in range(N):
        k = np.flatnonzero(a[:, d].reshape(-1) >= 0)
        m.append(table(k[::-1] if back else rng.permutation(k)))
    return {"send": np.stack([table(a[s].reshape(-1)) for s in range(N)]), "mine": np.stack(m), "prev": np.stack([m[(r - 1) % N] for r in range(N)])}
def setup_inputs(rng):
    return {"x": f(rng, N, 128, 4 * T), **lists(rng, counts(rng, even(N)))}
def setup_inputs_empty(rng):
    return {**setup_inputs(rng), **lists(rng, counts(rng, even(N - 1) + [0]))}
def setup_inputs_full(rng):
    return {**setup_inputs(rng), **lists(rng, counts(rng, [min(CAPP, max(0, T - k * CAPP)) for k in range(N)], 0))}
def setup_inputs_reversed(rng):
    return {**setup_inputs(rng), **lists(rng, counts(rng, even(N)), back=True)}
def setup_inputs_spread(rng):
    d = setup_inputs(rng); d["x"] = wide(rng, N, 128, 4 * T, cols=8); return d
def check_inputs(d):
    b = []
    v = np.abs(np.asarray(d["x"]).astype(np.float32))
    if not ((v == 0) | ((v >= 2.0 ** -30) & (v <= 2.0 ** 30))).all(): b.append("x")
    for r in range(N):
        c, m = entries(d["send"][r]), entries(d["mine"][r])
        if c.min() < -1 or not np.array_equal(np.sort(c[c >= 0]), np.arange(T)): b.append("send")
        arrived = np.concatenate([entries(d["send"][s])[r * CAPP:(r + 1) * CAPP] for s in range(N)])
        if not np.array_equal(np.sort(m), np.flatnonzero(arrived >= 0)): b.append("mine")
        if not np.array_equal(d["prev"][r], d["mine"][(r - 1) % N]): b.append("prev")
    return b
def reference(x, send, mine, prev):
    K = []
    for r in range(N):
        arrived = np.concatenate([cols(x[s], entries(send[s])[r * CAPP:(r + 1) * CAPP]) for s in range(N)], axis=1)
        K.append(cols(arrived, entries(mine[r])))
    Q = [mx_ref.quantize(t) for t in K]
    y = np.zeros((N, T, 2 * T), np.float32)
    for r in range(N):
        for p in range(T // 128):
            W = mx_ref.quantize(np.ascontiguousarray(K[r][:, 512 * p:512 * p + 512]))
            y[r, 128 * p:128 * p + 128, :T] = mx_ref.matmul(W, Q[r])
            y[r, 128 * p:128 * p + 128, T:] = mx_ref.matmul(W, Q[(r - 1) % N])
    return {"y": y}

@@ -1,0 +1,323 @@
+from concourse.bass import DstId, RemoteDMATransfer, IndirectOffsetOnAxis
+from concourse.mybir import dt, AluOpType, AxisListType, ActivationFunctionType
+
+N = 8
+CAPP = 48
+TC = 256
+SLOTS = N * CAPP
+TILE = SLOTS - CAPP
+PREV = 2 * TILE
+KW = PREV + SLOTS
+HALF = SLOTS // 2
+EMPTY = 1000.0
+
+SCRATCH = {
+    "xs": ("sbuf", [128, 4 * TC], "bfloat16"),
+    "h": ("sbuf", [128, 4 * SLOTS], "bfloat16"),
+    "sl": ("sbuf", [128, SLOTS // 16], "int32"),
+    "off": ("sbuf", [128, SLOTS // 16], "uint16"),
+    "kc": ("sbuf", [128, KW], "float8_e4m3fn_x4"),
+    "kp": ("sbuf", [128, KW], "uint8"),
+    "fc": ("sbuf", [128, 2 * CAPP], "float8_e4m3fn_x4"),
+    "fp": ("sbuf", [128, 2 * CAPP], "uint8"),
+    "ml": ("sbuf", [128, 32], "int32"),
+    "mf": ("sbuf", [128, 32], "float32"),
+    "step": ("sbuf", [128, 16 * 16], "float32"),
+    "acc": ("sbuf", [128, 16 * 16], "float32"),
+    "offo": ("sbuf", [128, 16], "uint16"),
+    "offp": ("sbuf", [128, 16], "uint16"),
+    "places": ("sbuf", [128, TC], "float32"),
+    "diag": ("sbuf", [128, SLOTS], "float32"),
+    "mask": ("sbuf", [128, SLOTS], "float32"),
+    "inv": ("sbuf", [128, SLOTS], "float32"),
+    "prod": ("sbuf", [128, SLOTS], "float32"),
+    "idxf": ("sbuf", [128, 4], "float32"),
+    "idx": ("sbuf", [128, 4], "int32"),
+    "wo": ("sbuf", [128, 3 * SLOTS], "float32"),
+    "wp": ("sbuf", [128, 3 * SLOTS], "float32"),
+    "res": ("sbuf", [128, 3 * 2 * TC], "float32"),
+    "ps": ("psum", [128, 8 * 512], "float32"),
+}
+SEMAPHORES = ["lds", "ldx", "ldl", "ldg", "gi", "v", "sa", "pe", "arr_same", "arr_cross", "hop_c", "hop_p", "out", "sc"]
+
+
+def split(engs, k):
+    n = len(engs) // k
+    return [sum(1 << e for e in engs[i * n:(i + 1) * n]) for i in range(k)]
+
+
+def bits(m):
+    return bin(m).count("1")
+
+
+def make_plan(T, topo):
+    cores = T.cores
+    same = [[q for q in range(N) if q != r and topo.same_plane(cores[r], cores[q])] for r in range(N)]
+    cross = [[q for q in range(N) if q != r and q not in same[r]] for r in range(N)]
+    carrier = {}
+    for s in range(N):
+        c0 = cores[s]
+        cls = sorted(same[s] + [s])
+        i = cls.index(s)
+        ports = []
+        for j, e in enumerate(cross[s]):
+            ports = [c for c in topo.cores_of(c0) if c != c0 and topo.may_write(c, cores[e])]
+            carrier[s, e] = ports[(i + j) % len(ports)]
+        spare = [c for c in topo.cores_of(c0) if c != c0 and c not in ports and topo.die(c) != topo.die(c0)]
+        for e in same[s]:
+            carrier[s, e] = spare[0] if e == cls[(i + 1) % len(cls)] else None
+    return same, cross, carrier
+
+
+def dst_of(topo, d, core):
+    rid, pid = topo.addr(d, core)
+    return [DstId(rid=rid, pnc=pid)]
+
+
+def block_orders(r, same, cross):
+    return cross[r] + same[r] + [r], [r] + same[r] + cross[r]
+
+
+def off_chip_masks(topo, src, dst, k):
+    return split(topo.engines(src, dst), k)
+
+
+def last_hop(g, T, topo, core, plan, s, e, codes, planes, col, masks, what):
+    same, cross, _ = plan
+    own, prev = block_orders(e, same, cross)
+    sem = T.sem.arr_same if s in same[e] else T.sem.arr_cross
+    d = dst_of(topo, T.cores[e], core)
+    tr = []
+    for part, at in ((0, PREV + CAPP * prev.index(s)), (1, CAPP * own.index(s))):
+        a = col + CAPP * part
+        if what == "codes":
+            src, dst = codes[:, a:a + CAPP].bitcast(dt.uint8), T.kc[:, at:at + CAPP].bitcast(dt.uint8)
+        else:
+            src, dst = planes[:, a:a + CAPP], T.kp[:, at:at + CAPP]
+        tr.append(RemoteDMATransfer(dst_ids=d, dma_engine_mask=masks[part], remote_sem=sem, src=src, dst=dst))
+    return tr
+
+
+def relay_program(g, core, T, topo, plan, s, e):
+    hop_engines = hop_masks(T, topo, plan, s)[e]
+    masks = off_chip_masks(topo, core, T.cores[e], 2)
+    for what, sem in (("codes", T.sem.hop_c), ("planes", T.sem.hop_p)):
+        g.wait_ge(sem, bits(hop_engines))
+        g.remote_dma_fused(last_hop(g, T, topo, core, plan, s, e, T.fc, T.fp, 0, masks, what), local_sem=T.sem.out)
+    g.wait_ge(T.sem.out, 2 * sum(bits(m) for m in masks))
+
+
+def hop_masks(T, topo, plan, s):
+    same, cross, carrier = plan
+    c0 = T.cores[s]
+    chip_engs = topo.engines(c0, carrier[s, cross[s][0]])
+    out = dict(zip(cross[s], split(chip_engs, len(cross[s]))))
+    for e in same[s]:
+        if carrier[s, e] is not None:
+            off = topo.engines(c0, T.cores[e])
+            out[e] = split([k for k in chip_engs if k not in off], 1)[0]
+    return out
+
+
+def direct_ranks(plan, s):
+    same, cross, carrier = plan
+    return [e for e in same[s] if carrier[s, e] is None]
+
+
+def direct_masks(T, topo, plan, s):
+    d = direct_ranks(plan, s)
+    m = split(topo.engines(T.cores[s], T.cores[d[0]]), 2 * len(d))
+    return {e: m[2 * k:2 * k + 2] for k, e in enumerate(d)}
+
+
+def arrivals(T, topo, plan, e):
+    same, cross, carrier = plan
+    n = []
+    for group in (same[e], cross[e]):
+        t = 0
+        for s in group:
+            c = carrier[s, e]
+            ms = direct_masks(T, topo, plan, s)[e] if c is None else off_chip_masks(topo, c, T.cores[e], 2)
+            t += 2 * sum(bits(m) for m in ms)
+        n.append(t)
+    return n
+
+
+def rank_program(g, core, T, topo):
+    plan = make_plan(T, topo)
+    rank = T.rank_of(core)
+    if rank is None:
+        for (s, e), c in sorted(plan[2].items()):
+            if c == core:
+                relay_program(g, core, T, topo, plan, s, e)
+        return
+    r = rank
+    same, cross, carrier = plan
+    sem = T.sem
+    nv, ns = [0], [0]
+    A = AluOpType
+    COPY = ActivationFunctionType.Copy
+
+    def V(ins):
+        ins.then_inc(sem.v, 1)
+        nv[0] += 1
+        return nv[0]
+
+    def S(ins):
+        ins.then_inc(sem.sa, 1)
+        ns[0] += 1
+        return ns[0]
+
+    def vw(n):
+        g.vector.wait_ge(sem.v, n)
+
+    g.sync.dma_start(T.xs[:], T.x[:]).then_inc(sem.ldx, 16)
+    for k in range(N):
+        q = g.sync if k < 3 else g.scalar
+        q.dma_start(T.sl[16 * k:16 * k + 16, :], T.send[:]).then_inc(sem.lds, 16)
+    g.dma_start(T.ml[112:128, 16:32], T.prev[:]).then_inc(sem.ldg, 16)
+    for k in range(N):
+        g.sync.dma_start(T.ml[16 * k:16 * k + 16, 0:16], T.mine[:]).then_inc(sem.ldl, 16)
+        if k < N - 1:
+            g.sync.dma_start(T.ml[16 * k:16 * k + 16, 16:32], T.prev[:]).then_inc(sem.ldl, 16)
+    g.iota(T.places[:], [[1, TC]], 0, 0, allow_small_or_imprecise_dtypes=True).then_inc(sem.gi, 1)
+    g.iota(T.diag[:], [[0, 3], [1, 128]], 0, -1, allow_small_or_imprecise_dtypes=True).then_inc(sem.gi, 1)
+
+    v_inv = V(g.vector.memset(T.inv[:], EMPTY))
+    g.vector.wait_ge(sem.lds, 16 * N)
+    w = SLOTS // 16
+    a = 3 * r
+    v_off = V(g.vector.tensor_scalar(T.off[:, 0:w - a], T.sl[:, a:w], 4.0, 0.0, A.mult, A.max))
+    if a:
+        v_off = V(g.vector.tensor_scalar(T.off[:, w - a:w], T.sl[:, 0:a], 4.0, 0.0, A.mult, A.max))
+
+    def win(t):
+        return T.xs[:, t:4 * TC].indirect(T.off[:, 0:w])
+
+    g.vector.wait_ge(sem.ldx, 16)
+    vw(v_off)
+    g.scalar.wait_ge(sem.ldx, 16)
+    g.scalar.wait_ge(sem.v, v_off)
+    for t in (0, 1):
+        v_h = V(g.vector.tensor_copy(T.h[:, t:4 * SLOTS:4], win(t)))
+    for t in (2, 3):
+        s_h = S(g.scalar.activation(T.h[:, t:4 * SLOTS:4], win(t), COPY))
+    g.vector.wait_ge(sem.sa, s_h)
+    vw(v_h)
+    v_q = V(g.vector.quantize_mx(T.kc[:, TILE:TILE + SLOTS], T.kp[:, TILE:TILE + SLOTS], T.h[:]))
+
+    def col(e):
+        return TILE + CAPP * ((e - 1 - r) % N)
+
+    hm = hop_masks(T, topo, plan, r)
+    dm = direct_masks(T, topo, plan, r)
+    sent = 0
+    g.wait_ge(sem.v, v_q)
+    via_same = [e for e in same[r] if carrier[r, e] is not None]
+    for group in (cross[r], via_same):
+        for what in ("codes", "planes"):
+            tr = []
+            for e in group:
+                b = col(e)
+                if what == "codes":
+                    src, dst, rs = T.kc[:, b:b + 2 * CAPP].bitcast(dt.uint8), T.fc[:, 0:2 * CAPP].bitcast(dt.uint8), sem.hop_c
+                else:
+                    src, dst, rs = T.kp[:, b:b + 2 * CAPP], T.fp[:, 0:2 * CAPP], sem.hop_p
+                tr.append(RemoteDMATransfer(dst_ids=dst_of(topo, carrier[r, e], core), dma_engine_mask=hm[e], remote_sem=rs,
+                                            src=src, dst=dst))
+                sent += bits(hm[e])
+            g.remote_dma_fused(tr, local_sem=sem.out)
+    for what in ("codes", "planes"):
+        tr = []
+        for e in direct_ranks(plan, r):
+            tr += last_hop(g, T, topo, core, plan, r, e, T.kc, T.kp, col(e), dm[e], what)
+            sent += sum(bits(m) for m in dm[e])
+        g.remote_dma_fused(tr, local_sem=sem.out)
+    g.wait_ge(sem.out, sent)
+
+    g.vector.wait_ge(sem.ldl, 16 * (2 * N - 1))
+    g.vector.wait_ge(sem.ldg, 16)
+    v_mf = V(g.vector.tensor_copy(T.mf[:], T.ml[:]))
+    vw(v_mf)
+    own, prev = block_orders(r, same, cross)
+    v_offs = []
+    for part, (order, out) in enumerate(((own, T.offo), (prev, T.offp))):
+        d = [float(CAPP * (order.index(s) - s)) for s in range(N)]
+        cur = T.mf[:, 16 * part:16 * part + 16]
+        steps = []
+        for s in range(1, N):
+            if d[s] != d[s - 1]:
+                k = 16 * (N * part + s)
+                v_s = V(g.vector.tensor_scalar(T.step[:, k:k + 16], T.mf[:, 16 * part:16 * part + 16], float(CAPP * s),
+                                               d[s] - d[s - 1], A.is_ge, A.mult))
+                steps.append((k, v_s))
+        for k, v_s in steps:
+            vw(nv[0])
+            V(g.vector.tensor_tensor(T.acc[:, k:k + 16], cur, T.step[:, k:k + 16], A.add))
+            cur = T.acc[:, k:k + 16]
+        vw(nv[0])
+        v_offs.append(V(g.vector.tensor_scalar(out[:], cur, d[0], 0.0, A.add, A.max)))
+    v_offo, v_offp = v_offs
+    g.vector.wait_ge(sem.gi, 2)
+    v_mask = V(g.vector.tensor_scalar(T.mask[:], T.diag[:], 0.0, None, A.is_equal))
+    vw(v_offo)
+    V(g.vector.tensor_copy(T.inv[:, 0:SLOTS].indirect(T.offo[:, 0:16]), T.places[:]))
+    vw(nv[0])
+    V(g.vector.tensor_tensor(T.prod[:], T.inv[:], T.mask[:], A.mult))
+    vw(nv[0])
+    for b in range(3):
+        V(g.vector.tensor_reduce(T.idxf[:, b:b + 1], T.prod[:, 128 * b:128 * b + 128], AxisListType.X, A.max))
+    vw(nv[0])
+    v_idx = V(g.vector.tensor_copy(T.idx[:, 0:3], T.idxf[:, 0:3]))
+
+    n_same, n_cross = arrivals(T, topo, plan, r)
+    npe = [0]
+
+    def mm(b, a, n):
+        i = npe[0]
+        g.tensor.matmul_mx(T.ps[:, 512 * i:512 * i + n], T.kc[:, 128 * b:128 * b + 128], T.kp[:, 128 * b:128 * b + 128],
+                           T.kc[:, a:a + n], T.kp[:, a:a + n], True, True).then_inc(sem.pe, 1)
+        npe[0] += 1
+
+    g.tensor.wait_ge(sem.v, v_q)
+    g.tensor.wait_ge(sem.arr_same, n_same)
+    mm(2, HALF, HALF)
+    mm(2, PREV, HALF)
+    g.tensor.wait_ge(sem.arr_cross, n_cross)
+    mm(2, 0, HALF)
+    mm(2, PREV + HALF, HALF)
+    for b in (1, 0):
+        mm(b, 0, SLOTS)
+        mm(b, PREV, SLOTS)
+
+    def v_copy(bank, at, n):
+        g.vector.wait_ge(sem.pe, bank + 1)
+        V(g.vector.tensor_copy(T.wo[:, at:at + n], T.ps[:, 512 * bank:512 * bank + n]))
+
+    def s_copy(bank, at, n):
+        g.scalar.wait_ge(sem.pe, bank + 1)
+        S(g.scalar.activation(T.wp[:, at:at + n], T.ps[:, 512 * bank:512 * bank + n], COPY))
+
+    g.scalar.wait_ge(sem.v, v_offp)
+    done = []
+    for i, b in enumerate((2, 1, 0)):
+        w0 = SLOTS * i
+        if i == 0:
+            v_copy(0, w0 + HALF, HALF)
+            s_copy(1, w0, HALF)
+            v_copy(2, w0, HALF)
+            s_copy(3, w0 + HALF, HALF)
+        else:
+            v_copy(2 + 2 * i, w0, SLOTS)
+            s_copy(3 + 2 * i, w0, SLOTS)
+        vw(nv[0])
+        V(g.vector.tensor_copy(T.res[:, 512 * i:512 * i + TC], T.wo[:, w0:w0 + SLOTS].indirect(T.offo[:, 0:16])))
+        g.scalar.wait_ge(sem.sa, ns[0])
+        S(g.scalar.activation(T.res[:, 512 * i + TC:512 * i + 512], T.wp[:, w0:w0 + SLOTS].indirect(T.offp[:, 0:16]), COPY))
+        done.append((b, nv[0], ns[0]))
+    for i, (b, dv, ds) in enumerate(done):
+        g.wait_ge(sem.v, dv)
+        g.wait_ge(sem.sa, ds)
+        g.indirect_dma_start(T.y[:], IndirectOffsetOnAxis(ap=T.idx[:, b:b + 1], axis=0), T.res[:, 512 * i:512 * i + 512], None,
+                             bounds_check=TC - 1, oob_is_err=False).then_inc(sem.sc, 16)
+    g.wait_ge(sem.sc, 48)

@@ -5,36 +5,54 @@ N = 8
 CAPP = 48
 TC = 256
 SLOTS = N * CAPP
-TILE = SLOTS - CAPP
-PREV = 2 * TILE
-KW = PREV + SLOTS
-HALF = SLOTS // 2
+PART = 3 * CAPP
+FIRST = 16
+XB = CAPP
+RUN1 = XB + 256
+TILE = RUN1 - FIRST
+RUN2 = TILE + SLOTS - CAPP
+PN = N * CAPP - CAPP
+ZB = RUN2 + PN
+EARLY = RUN2 + 5 * CAPP
+END = ZB + 128
+AGAIN = END - (CAPP - FIRST)
+KW = AGAIN + 128
+BLOCKS = (ZB, XB, XB + 128)
 EMPTY = 1000.0
+W = 768
+WZ = RUN1
+WP = RUN1 + 128
+NSTEP = 8
+OA = PART // 16
+OB = OA + 1
 
 SCRATCH = {
     "xs": ("sbuf", [128, 4 * TC], "bfloat16"),
     "h": ("sbuf", [128, 4 * SLOTS], "bfloat16"),
     "sl": ("sbuf", [128, SLOTS // 16], "int32"),
-    "off": ("sbuf", [128, SLOTS // 16], "uint16"),
+    "off": ("sbuf", [128, SLOTS // 16 + 2], "uint16"),
     "kc": ("sbuf", [128, KW], "float8_e4m3fn_x4"),
     "kp": ("sbuf", [128, KW], "uint8"),
     "fc": ("sbuf", [128, 2 * CAPP], "float8_e4m3fn_x4"),
     "fp": ("sbuf", [128, 2 * CAPP], "uint8"),
     "ml": ("sbuf", [128, 32], "int32"),
-    "mf": ("sbuf", [128, 32], "float32"),
-    "step": ("sbuf", [128, 16 * 16], "float32"),
-    "acc": ("sbuf", [128, 16 * 16], "float32"),
-    "offo": ("sbuf", [128, 16], "uint16"),
-    "offp": ("sbuf", [128, 16], "uint16"),
+    "step": ("sbuf", [128, 32 * NSTEP], "float32"),
+    "acc1": ("sbuf", [128, 16 * NSTEP], "float32"),
+    "acc2": ("sbuf", [128, 8 * NSTEP], "float32"),
+    "acc3": ("sbuf", [128, 4 * NSTEP], "float32"),
+    "offs": ("sbuf", [128, 32], "uint16"),
     "places": ("sbuf", [128, TC], "float32"),
-    "diag": ("sbuf", [128, SLOTS], "float32"),
-    "mask": ("sbuf", [128, SLOTS], "float32"),
     "inv": ("sbuf", [128, SLOTS], "float32"),
-    "prod": ("sbuf", [128, SLOTS], "float32"),
+    "part": ("sbuf", [128, 4], "int32"),
+    "offd": ("sbuf", [128, 4], "uint16"),
+    "lane": ("sbuf", [128, 48], "int32"),
+    "lanb": ("sbuf", [128, 48], "int32"),
+    "mask": ("sbuf", [128, 48], "float32"),
+    "dg": ("sbuf", [128, 48], "float32"),
+    "prod": ("sbuf", [128, 48], "float32"),
     "idxf": ("sbuf", [128, 4], "float32"),
     "idx": ("sbuf", [128, 4], "int32"),
-    "wo": ("sbuf", [128, 3 * SLOTS], "float32"),
-    "wp": ("sbuf", [128, 3 * SLOTS], "float32"),
+    "w": ("sbuf", [128, 3 * W], "float32"),
     "res": ("sbuf", [128, 3 * 2 * TC], "float32"),
     "ps": ("psum", [128, 8 * 512], "float32"),
 }
@@ -44,10 +62,6 @@ SEMAPHORES = ["lds", "ldx", "ldl", "ldg", "gi", "v", "sa", "pe", "arr_same", "ar
 def split(engs, k):
     n = len(engs) // k
     return [sum(1 << e for e in engs[i * n:(i + 1) * n]) for i in range(k)]
-
-
-def bits(m):
-    return bin(m).count("1")
 
 
 def make_plan(T, topo):
@@ -74,60 +88,74 @@ def dst_of(topo, d, core):
     return [DstId(rid=rid, pnc=pid)]
 
 
-def block_orders(r, same, cross):
-    return cross[r] + same[r] + [r], [r] + same[r] + cross[r]
+def layout(plan, r):
+    same, cross, carrier = plan
+    a, b = [s for s in same[r] if carrier[s, r] is None]
+    v = [s for s in same[r] if carrier[s, r] is not None][0]
+    prev = {a: 0, b: ZB - CAPP, v: ZB - 2 * CAPP, r: RUN2}
+    own = {a: XB, b: ZB, v: ZB + CAPP}
+    for k, m in enumerate(cross[r]):
+        prev[m] = RUN2 + CAPP * (k + 1)
+        own[m] = XB + CAPP * (k + 1)
+    return prev, own
 
 
-def off_chip_masks(topo, src, dst, k):
-    return split(topo.engines(src, dst), k)
-
-
-def last_hop(g, T, topo, core, plan, s, e, codes, planes, col, masks, what):
-    same, cross, _ = plan
-    own, prev = block_orders(e, same, cross)
+def last_hop(T, topo, core, plan, s, e, codes, planes, col, engs, what):
+    same, cross, carrier = plan
+    prev, own = layout(plan, e)
     sem = T.sem.arr_same if s in same[e] else T.sem.arr_cross
-    d = dst_of(topo, T.cores[e], core)
+    if own[s] == prev[s] + CAPP:
+        runs = [(0, prev[s], 2 * CAPP)]
+    else:
+        runs = [(0, prev[s], CAPP), (CAPP, own[s], CAPP)]
     tr = []
-    for part, at in ((0, PREV + CAPP * prev.index(s)), (1, CAPP * own.index(s))):
-        a = col + CAPP * part
+    for (at, to, n), m in zip(runs, split(engs, len(runs))):
+        a = col + at
         if what == "codes":
-            src, dst = codes[:, a:a + CAPP].bitcast(dt.uint8), T.kc[:, at:at + CAPP].bitcast(dt.uint8)
+            src, dst = codes[:, a:a + n].bitcast(dt.uint8), T.kc[:, to:to + n].bitcast(dt.uint8)
         else:
-            src, dst = planes[:, a:a + CAPP], T.kp[:, at:at + CAPP]
-        tr.append(RemoteDMATransfer(dst_ids=d, dma_engine_mask=masks[part], remote_sem=sem, src=src, dst=dst))
+            src, dst = planes[:, a:a + n], T.kp[:, to:to + n]
+        tr.append(RemoteDMATransfer(dst_ids=dst_of(topo, T.cores[e], core), dma_engine_mask=m, remote_sem=sem, src=src, dst=dst))
     return tr
 
 
-def relay_program(g, core, T, topo, plan, s, e):
-    hop_engines = hop_masks(T, topo, plan, s)[e]
-    masks = off_chip_masks(topo, core, T.cores[e], 2)
-    for what, sem in (("codes", T.sem.hop_c), ("planes", T.sem.hop_p)):
-        g.wait_ge(sem, bits(hop_engines))
-        g.remote_dma_fused(last_hop(g, T, topo, core, plan, s, e, T.fc, T.fp, 0, masks, what), local_sem=T.sem.out)
-    g.wait_ge(T.sem.out, 2 * sum(bits(m) for m in masks))
+def groups_of(plan, s):
+    same, cross, carrier = plan
+    first = [(s + 1) % N, (s + 2) % N]
+    return first, [e for e in cross[s] if e not in first], [e for e in same[s] if e not in first]
 
 
-def hop_masks(T, topo, plan, s):
+def hop_engines(T, topo, plan, s):
     same, cross, carrier = plan
     c0 = T.cores[s]
     chip_engs = topo.engines(c0, carrier[s, cross[s][0]])
-    out = dict(zip(cross[s], split(chip_engs, len(cross[s]))))
-    for e in same[s]:
+    low = topo.engines(c0, T.cores[[e for e in same[s] if carrier[s, e] is None][0]])
+    high = [k for k in chip_engs if k not in low]
+    first, far, near = groups_of(plan, s)
+    out = {}
+    a, b = first if first[0] in cross[s] else first[::-1]
+    out[a], out[b] = high, low
+    out[far[0]] = high
+    n = len(low) // (len(far) - 1)
+    for k, e in enumerate(far[1:]):
+        out[e] = low[n * k:n * k + n]
+    direct = [e for e in near if carrier[s, e] is None]
+    n = len(low) // len(direct)
+    for k, e in enumerate(direct):
+        out[e] = low[n * k:n * k + n]
+    for e in near:
         if carrier[s, e] is not None:
-            off = topo.engines(c0, T.cores[e])
-            out[e] = split([k for k in chip_engs if k not in off], 1)[0]
+            out[e] = high
     return out
 
 
-def direct_ranks(plan, s):
-    same, cross, carrier = plan
-    return [e for e in same[s] if carrier[s, e] is None]
-
-
-def direct_masks(T, topo, plan, s):
-    d = direct_ranks(plan, s)
-    m = split(topo.engines(T.cores[s], T.cores[d[0]]), 2 * len(d))
-    return {e: m[2 * k:2 * k + 2] for k, e in enumerate(d)}
+def relay_program(g, core, T, topo, plan, s, e):
+    n = len(hop_engines(T, topo, plan, s)[e])
+    engs = topo.engines(core, T.cores[e])
+    for what, sem in (("planes", T.sem.hop_p), ("codes", T.sem.hop_c)):
+        g.wait_ge(sem, n)
+        g.remote_dma_fused(last_hop(T, topo, core, plan, s, e, T.fc, T.fp, 0, engs, what), local_sem=T.sem.out)
+    g.wait_ge(T.sem.out, 2 * len(engs))
 
 
 def arrivals(T, topo, plan, e):
@@ -137,8 +165,7 @@ def arrivals(T, topo, plan, e):
         t = 0
         for s in group:
             c = carrier[s, e]
-            ms = direct_masks(T, topo, plan, s)[e] if c is None else off_chip_masks(topo, c, T.cores[e], 2)
-            t += 2 * sum(bits(m) for m in ms)
+            t += 2 * len(hop_engines(T, topo, plan, s)[e] if c is None else topo.engines(c, T.cores[e]))
         n.append(t)
     return n
 
@@ -180,144 +207,153 @@ def rank_program(g, core, T, topo):
         g.sync.dma_start(T.ml[16 * k:16 * k + 16, 0:16], T.mine[:]).then_inc(sem.ldl, 16)
         if k < N - 1:
             g.sync.dma_start(T.ml[16 * k:16 * k + 16, 16:32], T.prev[:]).then_inc(sem.ldl, 16)
+    g.iota(T.part[:, 0:4], [[128, 4]], 0, 1).then_inc(sem.gi, 1)
+    g.iota(T.lane[:], [[0, 3], [-1, 16]], 0, 1).then_inc(sem.gi, 1)
     g.iota(T.places[:], [[1, TC]], 0, 0, allow_small_or_imprecise_dtypes=True).then_inc(sem.gi, 1)
-    g.iota(T.diag[:], [[0, 3], [1, 128]], 0, -1, allow_small_or_imprecise_dtypes=True).then_inc(sem.gi, 1)
 
-    v_inv = V(g.vector.memset(T.inv[:], EMPTY))
+    V(g.vector.memset(T.inv[:], EMPTY))
+    v_fill = V(g.vector.memset(T.step[:], 0.0))
     g.vector.wait_ge(sem.lds, 16 * N)
     w = SLOTS // 16
-    a = 3 * r
-    v_off = V(g.vector.tensor_scalar(T.off[:, 0:w - a], T.sl[:, a:w], 4.0, 0.0, A.mult, A.max))
-    if a:
-        v_off = V(g.vector.tensor_scalar(T.off[:, w - a:w], T.sl[:, 0:a], 4.0, 0.0, A.mult, A.max))
-
-    def win(t):
-        return T.xs[:, t:4 * TC].indirect(T.off[:, 0:w])
+    wrap = w - 3 * r
+    cuts = sorted({0, OA, w} | ({wrap} if r else set()))
+    for lo, hi in zip(cuts, cuts[1:]):
+        src = (lo + 3 * r) % w
+        to = lo if lo < OA else lo + OB - OA
+        v_off = V(g.vector.tensor_scalar(T.off[:, to:to + hi - lo], T.sl[:, src:src + hi - lo], 4.0, 0.0, A.mult, A.max))
 
     g.vector.wait_ge(sem.ldx, 16)
     vw(v_off)
     g.scalar.wait_ge(sem.ldx, 16)
     g.scalar.wait_ge(sem.v, v_off)
-    for t in (0, 1):
-        v_h = V(g.vector.tensor_copy(T.h[:, t:4 * SLOTS:4], win(t)))
-    for t in (2, 3):
-        s_h = S(g.scalar.activation(T.h[:, t:4 * SLOTS:4], win(t), COPY))
-    g.vector.wait_ge(sem.sa, s_h)
-    vw(v_h)
-    v_q = V(g.vector.quantize_mx(T.kc[:, TILE:TILE + SLOTS], T.kp[:, TILE:TILE + SLOTS], T.h[:]))
+    v_qs = []
+    for c0, c1, o0, o1 in ((0, PART, 0, OA), (PART, SLOTS, OB, w + 1)):
+        for t in (0, 1):
+            v_h = V(g.vector.tensor_copy(T.h[:, 4 * c0 + t:4 * c1:4], T.xs[:, t:4 * TC].indirect(T.off[:, o0:o1])))
+        for t in (2, 3):
+            s_h = S(g.scalar.activation(T.h[:, 4 * c0 + t:4 * c1:4], T.xs[:, t:4 * TC].indirect(T.off[:, o0:o1]), COPY))
+        g.vector.wait_ge(sem.sa, s_h)
+        vw(v_h)
+        v_qs.append(V(g.vector.quantize_mx(T.kc[:, TILE + c0:TILE + c1], T.kp[:, TILE + c0:TILE + c1], T.h[:, 4 * c0:4 * c1])))
+    v_q2 = V(g.vector.quantize_mx(T.kc[:, AGAIN:AGAIN + 128], T.kp[:, AGAIN:AGAIN + 128],
+                                  T.h[:, 4 * FIRST:4 * FIRST + 512]))
 
-    def col(e):
-        return TILE + CAPP * ((e - 1 - r) % N)
-
-    hm = hop_masks(T, topo, plan, r)
-    dm = direct_masks(T, topo, plan, r)
+    he = hop_engines(T, topo, plan, r)
     sent = 0
-    g.wait_ge(sem.v, v_q)
-    via_same = [e for e in same[r] if carrier[r, e] is not None]
-    for group in (cross[r], via_same):
-        for what in ("codes", "planes"):
+    for i, group in enumerate(groups_of(plan, r)):
+        if i < 2:
+            g.wait_ge(sem.v, v_qs[i])
+        for what in ("planes", "codes"):
             tr = []
             for e in group:
-                b = col(e)
+                b = TILE + CAPP * ((e - 1 - r) % N)
+                sent += len(he[e])
+                if carrier[r, e] is None:
+                    tr += last_hop(T, topo, core, plan, r, e, T.kc, T.kp, b, he[e], what)
+                    continue
                 if what == "codes":
                     src, dst, rs = T.kc[:, b:b + 2 * CAPP].bitcast(dt.uint8), T.fc[:, 0:2 * CAPP].bitcast(dt.uint8), sem.hop_c
                 else:
                     src, dst, rs = T.kp[:, b:b + 2 * CAPP], T.fp[:, 0:2 * CAPP], sem.hop_p
-                tr.append(RemoteDMATransfer(dst_ids=dst_of(topo, carrier[r, e], core), dma_engine_mask=hm[e], remote_sem=rs,
-                                            src=src, dst=dst))
-                sent += bits(hm[e])
+                tr.append(RemoteDMATransfer(dst_ids=dst_of(topo, carrier[r, e], core), dma_engine_mask=split(he[e], 1)[0],
+                                            remote_sem=rs, src=src, dst=dst))
             g.remote_dma_fused(tr, local_sem=sem.out)
-    for what in ("codes", "planes"):
-        tr = []
-        for e in direct_ranks(plan, r):
-            tr += last_hop(g, T, topo, core, plan, r, e, T.kc, T.kp, col(e), dm[e], what)
-            sent += sum(bits(m) for m in dm[e])
-        g.remote_dma_fused(tr, local_sem=sem.out)
-    g.wait_ge(sem.out, sent)
 
+    at_prev, at_own = layout(plan, r)
+    own = {s: (c - XB if c < TILE else c - ZB + 256) for s, c in at_own.items()}
+    own[r] = 256 - FIRST
+    prev = {s: (c if c < RUN1 else c - RUN2 + WP) for s, c in at_prev.items()}
+    jump = 128 - (CAPP - FIRST)
     g.vector.wait_ge(sem.ldl, 16 * (2 * N - 1))
     g.vector.wait_ge(sem.ldg, 16)
-    v_mf = V(g.vector.tensor_copy(T.mf[:], T.ml[:]))
-    vw(v_mf)
-    own, prev = block_orders(r, same, cross)
-    v_offs = []
-    for part, (order, out) in enumerate(((own, T.offo), (prev, T.offp))):
-        d = [float(CAPP * (order.index(s) - s)) for s in range(N)]
-        cur = T.mf[:, 16 * part:16 * part + 16]
+    vw(v_fill)
+    for part, pos in ((0, own), (1, prev)):
+        src = T.ml[:, 16 * part:16 * part + 16]
+        cur = pos[0]
         steps = []
-        for s in range(1, N):
-            if d[s] != d[s - 1]:
-                k = 16 * (N * part + s)
-                v_s = V(g.vector.tensor_scalar(T.step[:, k:k + 16], T.mf[:, 16 * part:16 * part + 16], float(CAPP * s),
-                                               d[s] - d[s - 1], A.is_ge, A.mult))
-                steps.append((k, v_s))
-        for k, v_s in steps:
-            vw(nv[0])
-            V(g.vector.tensor_tensor(T.acc[:, k:k + 16], cur, T.step[:, k:k + 16], A.add))
-            cur = T.acc[:, k:k + 16]
-        vw(nv[0])
-        v_offs.append(V(g.vector.tensor_scalar(out[:], cur, d[0], 0.0, A.add, A.max)))
-    v_offo, v_offp = v_offs
-    g.vector.wait_ge(sem.gi, 2)
-    v_mask = V(g.vector.tensor_scalar(T.mask[:], T.diag[:], 0.0, None, A.is_equal))
-    vw(v_offo)
-    V(g.vector.tensor_copy(T.inv[:, 0:SLOTS].indirect(T.offo[:, 0:16]), T.places[:]))
+        for s in range(N):
+            if s and pos[s] - CAPP * s != cur:
+                steps.append((CAPP * s, pos[s] - CAPP * s - cur))
+                cur = pos[s] - CAPP * s
+            if part == 0 and s == r:
+                steps.append((CAPP * s + FIRST, jump))
+                cur += jump
+        V(g.vector.tensor_scalar(T.step[:, 16 * part:16 * part + 16], src, float(pos[0]), None, A.add))
+        for k, (at, d) in enumerate(steps):
+            c = 32 * (k + 1) + 16 * part
+            V(g.vector.tensor_scalar(T.step[:, c:c + 16], src, float(at), float(d), A.is_ge, A.mult))
     vw(nv[0])
-    V(g.vector.tensor_tensor(T.prod[:], T.inv[:], T.mask[:], A.mult))
+    V(g.vector.tensor_tensor(T.acc1[:], T.step[:, 0:128], T.step[:, 128:256], A.add))
+    g.vector.wait_ge(sem.gi, 3)
+    V(g.vector.tensor_copy(T.offd[:], T.part[:]))
+    V(g.vector.tensor_scalar(T.lanb[:], T.lane[:], 15, None, A.bitwise_and))
+    vw(nv[0])
+    V(g.vector.tensor_tensor(T.acc2[:], T.acc1[:, 0:64], T.acc1[:, 64:128], A.add))
+    V(g.vector.tensor_scalar(T.mask[:], T.lanb[:], 0.0, None, A.is_equal))
+    vw(nv[0])
+    V(g.vector.tensor_tensor(T.acc3[:], T.acc2[:, 0:32], T.acc2[:, 32:64], A.add))
+    vw(nv[0])
+    v_offs = V(g.vector.tensor_scalar(T.offs[:], T.acc3[:], 0.0, None, A.max))
+    vw(v_offs)
+    V(g.vector.tensor_copy(T.inv[:, 0:SLOTS].indirect(T.offs[:, 0:16]), T.places[:]))
+    vw(nv[0])
+    V(g.vector.tensor_copy(T.dg[:], T.inv[:, 0:SLOTS].indirect(T.offd[:, 0:3])))
+    vw(nv[0])
+    V(g.vector.tensor_tensor(T.prod[:], T.dg[:], T.mask[:], A.mult))
     vw(nv[0])
     for b in range(3):
-        V(g.vector.tensor_reduce(T.idxf[:, b:b + 1], T.prod[:, 128 * b:128 * b + 128], AxisListType.X, A.max))
+        V(g.vector.tensor_reduce(T.idxf[:, b:b + 1], T.prod[:, 16 * b:16 * b + 16], AxisListType.X, A.max))
     vw(nv[0])
     v_idx = V(g.vector.tensor_copy(T.idx[:, 0:3], T.idxf[:, 0:3]))
 
     n_same, n_cross = arrivals(T, topo, plan, r)
     npe = [0]
 
-    def mm(b, a, n):
+    def mm(b, lo, hi):
         i = npe[0]
-        g.tensor.matmul_mx(T.ps[:, 512 * i:512 * i + n], T.kc[:, 128 * b:128 * b + 128], T.kp[:, 128 * b:128 * b + 128],
-                           T.kc[:, a:a + n], T.kp[:, a:a + n], True, True).then_inc(sem.pe, 1)
+        g.tensor.matmul_mx(T.ps[:, 512 * i:512 * i + hi - lo], T.kc[:, b:b + 128], T.kp[:, b:b + 128],
+                           T.kc[:, lo:hi], T.kp[:, lo:hi], True, True).then_inc(sem.pe, 1)
         npe[0] += 1
 
-    g.tensor.wait_ge(sem.v, v_q)
+    g.tensor.wait_ge(sem.v, v_q2)
     g.tensor.wait_ge(sem.arr_same, n_same)
-    mm(2, HALF, HALF)
-    mm(2, PREV, HALF)
+    mm(BLOCKS[0], EARLY, END)
     g.tensor.wait_ge(sem.arr_cross, n_cross)
-    mm(2, 0, HALF)
-    mm(2, PREV + HALF, HALF)
-    for b in (1, 0):
-        mm(b, 0, SLOTS)
-        mm(b, PREV, SLOTS)
+    mm(BLOCKS[0], 0, RUN1)
+    mm(BLOCKS[0], RUN2, EARLY)
+    for b in BLOCKS[1:]:
+        mm(b, 0, RUN1)
+        mm(b, RUN2, END)
 
-    def v_copy(bank, at, n):
-        g.vector.wait_ge(sem.pe, bank + 1)
-        V(g.vector.tensor_copy(T.wo[:, at:at + n], T.ps[:, 512 * bank:512 * bank + n]))
-
-    def s_copy(bank, at, n):
+    def s_copy(bank, at, lo, n):
         g.scalar.wait_ge(sem.pe, bank + 1)
-        S(g.scalar.activation(T.wp[:, at:at + n], T.ps[:, 512 * bank:512 * bank + n], COPY))
+        return S(g.scalar.activation(T.w[:, at:at + n], T.ps[:, 512 * bank + lo:512 * bank + lo + n], COPY))
 
-    g.scalar.wait_ge(sem.v, v_offp)
     done = []
-    for i, b in enumerate((2, 1, 0)):
-        w0 = SLOTS * i
+    for i in range(3):
+        o = W * i
+        bank = 2 * i + 1
         if i == 0:
-            v_copy(0, w0 + HALF, HALF)
-            s_copy(1, w0, HALF)
-            v_copy(2, w0, HALF)
-            s_copy(3, w0 + HALF, HALF)
+            s_z = s_copy(0, o + WZ, ZB - EARLY, 128)
+            s_copy(0, o + WP + EARLY - RUN2, 0, ZB - EARLY)
+            s_p = s_copy(2, o + WP, 0, EARLY - RUN2)
         else:
-            v_copy(2 + 2 * i, w0, SLOTS)
-            s_copy(3 + 2 * i, w0, SLOTS)
-        vw(nv[0])
-        V(g.vector.tensor_copy(T.res[:, 512 * i:512 * i + TC], T.wo[:, w0:w0 + SLOTS].indirect(T.offo[:, 0:16])))
-        g.scalar.wait_ge(sem.sa, ns[0])
-        S(g.scalar.activation(T.res[:, 512 * i + TC:512 * i + 512], T.wp[:, w0:w0 + SLOTS].indirect(T.offp[:, 0:16]), COPY))
-        done.append((b, nv[0], ns[0]))
-    for i, (b, dv, ds) in enumerate(done):
+            s_z = s_copy(bank + 1, o + WZ, PN, 128)
+            s_p = s_copy(bank + 1, o + WP, 0, PN)
+        g.vector.wait_ge(sem.pe, bank + 1)
+        v_c = V(g.vector.tensor_copy(T.w[:, o:o + RUN1], T.ps[:, 512 * bank:512 * bank + RUN1]))
+        g.vector.wait_ge(sem.sa, s_z)
+        vw(v_c)
+        v_g = V(g.vector.tensor_copy(T.res[:, 512 * i:512 * i + TC], T.w[:, o + XB:o + XB + SLOTS].indirect(T.offs[:, 0:16])))
+        g.scalar.wait_ge(sem.sa, s_p)
+        g.scalar.wait_ge(sem.v, v_c)
+        s_g = S(g.scalar.activation(T.res[:, 512 * i + TC:512 * i + 512], T.w[:, o:o + W].indirect(T.offs[:, 16:32]), COPY))
+        done.append((v_g, s_g))
+    for i, (dv, ds) in enumerate(done):
+        b = (2, 0, 1)[i]
         g.wait_ge(sem.v, dv)
         g.wait_ge(sem.sa, ds)
         g.indirect_dma_start(T.y[:], IndirectOffsetOnAxis(ap=T.idx[:, b:b + 1], axis=0), T.res[:, 512 * i:512 * i + 512], None,
                              bounds_check=TC - 1, oob_is_err=False).then_inc(sem.sc, 16)
+    g.wait_ge(sem.out, sent)
     g.wait_ge(sem.sc, 48)

from concourse.bass import DstId, RemoteDMATransfer, IndirectOffsetOnAxis
from concourse.mybir import dt, AluOpType, AxisListType, ActivationFunctionType

N = 8
CAPP = 48
TC = 256
SLOTS = N * CAPP
PART = 3 * CAPP
FIRST = 16
XB = CAPP
RUN1 = XB + 256
TILE = RUN1 - FIRST
RUN2 = TILE + SLOTS - CAPP
PN = N * CAPP - CAPP
ZB = RUN2 + PN
EARLY = RUN2 + 5 * CAPP
END = ZB + 128
AGAIN = END - (CAPP - FIRST)
KW = AGAIN + 128
BLOCKS = (ZB, XB, XB + 128)
EMPTY = 1000.0
W = 768
WZ = RUN1
WP = RUN1 + 128
NSTEP = 8
OA = PART // 16
OB = OA + 1

SCRATCH = {
    "xs": ("sbuf", [128, 4 * TC], "bfloat16"),
    "h": ("sbuf", [128, 4 * SLOTS], "bfloat16"),
    "sl": ("sbuf", [128, SLOTS // 16], "int32"),
    "off": ("sbuf", [128, SLOTS // 16 + 2], "uint16"),
    "kc": ("sbuf", [128, KW], "float8_e4m3fn_x4"),
    "kp": ("sbuf", [128, KW], "uint8"),
    "fc": ("sbuf", [128, 2 * CAPP], "float8_e4m3fn_x4"),
    "fp": ("sbuf", [128, 2 * CAPP], "uint8"),
    "ml": ("sbuf", [128, 32], "int32"),
    "step": ("sbuf", [128, 32 * NSTEP], "float32"),
    "acc1": ("sbuf", [128, 16 * NSTEP], "float32"),
    "acc2": ("sbuf", [128, 8 * NSTEP], "float32"),
    "acc3": ("sbuf", [128, 4 * NSTEP], "float32"),
    "offs": ("sbuf", [128, 32], "uint16"),
    "places": ("sbuf", [128, TC], "float32"),
    "inv": ("sbuf", [128, SLOTS], "float32"),
    "part": ("sbuf", [128, 4], "int32"),
    "offd": ("sbuf", [128, 4], "uint16"),
    "lane": ("sbuf", [128, 48], "int32"),
    "lanb": ("sbuf", [128, 48], "int32"),
    "mask": ("sbuf", [128, 48], "float32"),
    "dg": ("sbuf", [128, 48], "float32"),
    "prod": ("sbuf", [128, 48], "float32"),
    "idxf": ("sbuf", [128, 4], "float32"),
    "idx": ("sbuf", [128, 4], "int32"),
    "w": ("sbuf", [128, 3 * W], "float32"),
    "res": ("sbuf", [128, 3 * 2 * TC], "float32"),
    "ps": ("psum", [128, 8 * 512], "float32"),
}
SEMAPHORES = ["lds", "ldx", "ldl", "ldg", "gi", "v", "sa", "pe", "arr_same", "arr_cross", "hop_c", "hop_p", "out", "sc"]


def split(engs, k):
    n = len(engs) // k
    return [sum(1 << e for e in engs[i * n:(i + 1) * n]) for i in range(k)]


def make_plan(T, topo):
    cores = T.cores
    same = [[q for q in range(N) if q != r and topo.same_plane(cores[r], cores[q])] for r in range(N)]
    cross = [[q for q in range(N) if q != r and q not in same[r]] for r in range(N)]
    carrier = {}
    for s in range(N):
        c0 = cores[s]
        cls = sorted(same[s] + [s])
        i = cls.index(s)
        ports = []
        for j, e in enumerate(cross[s]):
            ports = [c for c in topo.cores_of(c0) if c != c0 and topo.may_write(c, cores[e])]
            carrier[s, e] = ports[(i + j) % len(ports)]
        spare = [c for c in topo.cores_of(c0) if c != c0 and c not in ports and topo.die(c) != topo.die(c0)]
        for e in same[s]:
            carrier[s, e] = spare[0] if e == cls[(i + 1) % len(cls)] else None
    return same, cross, carrier


def dst_of(topo, d, core):
    rid, pid = topo.addr(d, core)
    return [DstId(rid=rid, pnc=pid)]


def layout(plan, r):
    same, cross, carrier = plan
    a, b = [s for s in same[r] if carrier[s, r] is None]
    v = [s for s in same[r] if carrier[s, r] is not None][0]
    prev = {a: 0, b: ZB - CAPP, v: ZB - 2 * CAPP, r: RUN2}
    own = {a: XB, b: ZB, v: ZB + CAPP}
    for k, m in enumerate(cross[r]):
        prev[m] = RUN2 + CAPP * (k + 1)
        own[m] = XB + CAPP * (k + 1)
    return prev, own


def last_hop(T, topo, core, plan, s, e, codes, planes, col, engs, what):
    same, cross, carrier = plan
    prev, own = layout(plan, e)
    sem = T.sem.arr_same if s in same[e] else T.sem.arr_cross
    if own[s] == prev[s] + CAPP:
        runs = [(0, prev[s], 2 * CAPP)]
    else:
        runs = [(0, prev[s], CAPP), (CAPP, own[s], CAPP)]
    tr = []
    for (at, to, n), m in zip(runs, split(engs, len(runs))):
        a = col + at
        if what == "codes":
            src, dst = codes[:, a:a + n].bitcast(dt.uint8), T.kc[:, to:to + n].bitcast(dt.uint8)
        else:
            src, dst = planes[:, a:a + n], T.kp[:, to:to + n]
        tr.append(RemoteDMATransfer(dst_ids=dst_of(topo, T.cores[e], core), dma_engine_mask=m, remote_sem=sem, src=src, dst=dst))
    return tr


def groups_of(plan, s):
    same, cross, carrier = plan
    first = [(s + 1) % N, (s + 2) % N]
    return first, [e for e in cross[s] if e not in first], [e for e in same[s] if e not in first]


def hop_engines(T, topo, plan, s):
    same, cross, carrier = plan
    c0 = T.cores[s]
    chip_engs = topo.engines(c0, carrier[s, cross[s][0]])
    low = topo.engines(c0, T.cores[[e for e in same[s] if carrier[s, e] is None][0]])
    high = [k for k in chip_engs if k not in low]
    first, far, near = groups_of(plan, s)
    out = {}
    a, b = first if first[0] in cross[s] else first[::-1]
    out[a], out[b] = high, low
    out[far[0]] = high
    n = len(low) // (len(far) - 1)
    for k, e in enumerate(far[1:]):
        out[e] = low[n * k:n * k + n]
    direct = [e for e in near if carrier[s, e] is None]
    n = len(low) // len(direct)
    for k, e in enumerate(direct):
        out[e] = low[n * k:n * k + n]
    for e in near:
        if carrier[s, e] is not None:
            out[e] = high
    return out


def relay_program(g, core, T, topo, plan, s, e):
    n = len(hop_engines(T, topo, plan, s)[e])
    engs = topo.engines(core, T.cores[e])
    for what, sem in (("planes", T.sem.hop_p), ("codes", T.sem.hop_c)):
        g.wait_ge(sem, n)
        g.remote_dma_fused(last_hop(T, topo, core, plan, s, e, T.fc, T.fp, 0, engs, what), local_sem=T.sem.out)
    g.wait_ge(T.sem.out, 2 * len(engs))


def arrivals(T, topo, plan, e):
    same, cross, carrier = plan
    n = []
    for group in (same[e], cross[e]):
        t = 0
        for s in group:
            c = carrier[s, e]
            t += 2 * len(hop_engines(T, topo, plan, s)[e] if c is None else topo.engines(c, T.cores[e]))
        n.append(t)
    return n


def rank_program(g, core, T, topo):
    plan = make_plan(T, topo)
    rank = T.rank_of(core)
    if rank is None:
        for (s, e), c in sorted(plan[2].items()):
            if c == core:
                relay_program(g, core, T, topo, plan, s, e)
        return
    r = rank
    same, cross, carrier = plan
    sem = T.sem
    nv, ns = [0], [0]
    A = AluOpType
    COPY = ActivationFunctionType.Copy

    def V(ins):
        ins.then_inc(sem.v, 1)
        nv[0] += 1
        return nv[0]

    def S(ins):
        ins.then_inc(sem.sa, 1)
        ns[0] += 1
        return ns[0]

    def vw(n):
        g.vector.wait_ge(sem.v, n)

    g.sync.dma_start(T.xs[:], T.x[:]).then_inc(sem.ldx, 16)
    for k in range(N):
        q = g.sync if k < 3 else g.scalar
        q.dma_start(T.sl[16 * k:16 * k + 16, :], T.send[:]).then_inc(sem.lds, 16)
    g.dma_start(T.ml[112:128, 16:32], T.prev[:]).then_inc(sem.ldg, 16)
    for k in range(N):
        g.sync.dma_start(T.ml[16 * k:16 * k + 16, 0:16], T.mine[:]).then_inc(sem.ldl, 16)
        if k < N - 1:
            g.sync.dma_start(T.ml[16 * k:16 * k + 16, 16:32], T.prev[:]).then_inc(sem.ldl, 16)
    g.iota(T.part[:, 0:4], [[128, 4]], 0, 1).then_inc(sem.gi, 1)
    g.iota(T.lane[:], [[0, 3], [-1, 16]], 0, 1).then_inc(sem.gi, 1)
    g.iota(T.places[:], [[1, TC]], 0, 0, allow_small_or_imprecise_dtypes=True).then_inc(sem.gi, 1)

    V(g.vector.memset(T.inv[:], EMPTY))
    v_fill = V(g.vector.memset(T.step[:], 0.0))
    g.vector.wait_ge(sem.lds, 16 * N)
    w = SLOTS // 16
    wrap = w - 3 * r
    cuts = sorted({0, OA, w} | ({wrap} if r else set()))
    for lo, hi in zip(cuts, cuts[1:]):
        src = (lo + 3 * r) % w
        to = lo if lo < OA else lo + OB - OA
        v_off = V(g.vector.tensor_scalar(T.off[:, to:to + hi - lo], T.sl[:, src:src + hi - lo], 4.0, 0.0, A.mult, A.max))

    g.vector.wait_ge(sem.ldx, 16)
    vw(v_off)
    g.scalar.wait_ge(sem.ldx, 16)
    g.scalar.wait_ge(sem.v, v_off)
    v_qs = []
    for c0, c1, o0, o1 in ((0, PART, 0, OA), (PART, SLOTS, OB, w + 1)):
        for t in (0, 1):
            v_h = V(g.vector.tensor_copy(T.h[:, 4 * c0 + t:4 * c1:4], T.xs[:, t:4 * TC].indirect(T.off[:, o0:o1])))
        for t in (2, 3):
            s_h = S(g.scalar.activation(T.h[:, 4 * c0 + t:4 * c1:4], T.xs[:, t:4 * TC].indirect(T.off[:, o0:o1]), COPY))
        g.vector.wait_ge(sem.sa, s_h)
        vw(v_h)
        v_qs.append(V(g.vector.quantize_mx(T.kc[:, TILE + c0:TILE + c1], T.kp[:, TILE + c0:TILE + c1], T.h[:, 4 * c0:4 * c1])))
    v_q2 = V(g.vector.quantize_mx(T.kc[:, AGAIN:AGAIN + 128], T.kp[:, AGAIN:AGAIN + 128],
                                  T.h[:, 4 * FIRST:4 * FIRST + 512]))

    he = hop_engines(T, topo, plan, r)
    sent = 0
    for i, group in enumerate(groups_of(plan, r)):
        if i < 2:
            g.wait_ge(sem.v, v_qs[i])
        for what in ("planes", "codes"):
            tr = []
            for e in group:
                b = TILE + CAPP * ((e - 1 - r) % N)
                sent += len(he[e])
                if carrier[r, e] is None:
                    tr += last_hop(T, topo, core, plan, r, e, T.kc, T.kp, b, he[e], what)
                    continue
                if what == "codes":
                    src, dst, rs = T.kc[:, b:b + 2 * CAPP].bitcast(dt.uint8), T.fc[:, 0:2 * CAPP].bitcast(dt.uint8), sem.hop_c
                else:
                    src, dst, rs = T.kp[:, b:b + 2 * CAPP], T.fp[:, 0:2 * CAPP], sem.hop_p
                tr.append(RemoteDMATransfer(dst_ids=dst_of(topo, carrier[r, e], core), dma_engine_mask=split(he[e], 1)[0],
                                            remote_sem=rs, src=src, dst=dst))
            g.remote_dma_fused(tr, local_sem=sem.out)

    at_prev, at_own = layout(plan, r)
    own = {s: (c - XB if c < TILE else c - ZB + 256) for s, c in at_own.items()}
    own[r] = 256 - FIRST
    prev = {s: (c if c < RUN1 else c - RUN2 + WP) for s, c in at_prev.items()}
    jump = 128 - (CAPP - FIRST)
    g.vector.wait_ge(sem.ldl, 16 * (2 * N - 1))
    g.vector.wait_ge(sem.ldg, 16)
    vw(v_fill)
    for part, pos in ((0, own), (1, prev)):
        src = T.ml[:, 16 * part:16 * part + 16]
        cur = pos[0]
        steps = []
        for s in range(N):
            if s and pos[s] - CAPP * s != cur:
                steps.append((CAPP * s, pos[s] - CAPP * s - cur))
                cur = pos[s] - CAPP * s
            if part == 0 and s == r:
                steps.append((CAPP * s + FIRST, jump))
                cur += jump
        V(g.vector.tensor_scalar(T.step[:, 16 * part:16 * part + 16], src, float(pos[0]), None, A.add))
        for k, (at, d) in enumerate(steps):
            c = 32 * (k + 1) + 16 * part
            V(g.vector.tensor_scalar(T.step[:, c:c + 16], src, float(at), float(d), A.is_ge, A.mult))
    vw(nv[0])
    V(g.vector.tensor_tensor(T.acc1[:], T.step[:, 0:128], T.step[:, 128:256], A.add))
    g.vector.wait_ge(sem.gi, 3)
    V(g.vector.tensor_copy(T.offd[:], T.part[:]))
    V(g.vector.tensor_scalar(T.lanb[:], T.lane[:], 15, None, A.bitwise_and))
    vw(nv[0])
    V(g.vector.tensor_tensor(T.acc2[:], T.acc1[:, 0:64], T.acc1[:, 64:128], A.add))
    V(g.vector.tensor_scalar(T.mask[:], T.lanb[:], 0.0, None, A.is_equal))
    vw(nv[0])
    V(g.vector.tensor_tensor(T.acc3[:], T.acc2[:, 0:32], T.acc2[:, 32:64], A.add))
    vw(nv[0])
    v_offs = V(g.vector.tensor_scalar(T.offs[:], T.acc3[:], 0.0, None, A.max))
    vw(v_offs)
    V(g.vector.tensor_copy(T.inv[:, 0:SLOTS].indirect(T.offs[:, 0:16]), T.places[:]))
    vw(nv[0])
    V(g.vector.tensor_copy(T.dg[:], T.inv[:, 0:SLOTS].indirect(T.offd[:, 0:3])))
    vw(nv[0])
    V(g.vector.tensor_tensor(T.prod[:], T.dg[:], T.mask[:], A.mult))
    vw(nv[0])
    for b in range(3):
        V(g.vector.tensor_reduce(T.idxf[:, b:b + 1], T.prod[:, 16 * b:16 * b + 16], AxisListType.X, A.max))
    vw(nv[0])
    v_idx = V(g.vector.tensor_copy(T.idx[:, 0:3], T.idxf[:, 0:3]))

    n_same, n_cross = arrivals(T, topo, plan, r)
    npe = [0]

    def mm(b, lo, hi):
        i = npe[0]
        g.tensor.matmul_mx(T.ps[:, 512 * i:512 * i + hi - lo], T.kc[:, b:b + 128], T.kp[:, b:b + 128],
                           T.kc[:, lo:hi], T.kp[:, lo:hi], True, True).then_inc(sem.pe, 1)
        npe[0] += 1

    g.tensor.wait_ge(sem.v, v_q2)
    g.tensor.wait_ge(sem.arr_same, n_same)
    mm(BLOCKS[0], EARLY, END)
    g.tensor.wait_ge(sem.arr_cross, n_cross)
    mm(BLOCKS[0], 0, RUN1)
    mm(BLOCKS[0], RUN2, EARLY)
    for b in BLOCKS[1:]:
        mm(b, 0, RUN1)
        mm(b, RUN2, END)

    def s_copy(bank, at, lo, n):
        g.scalar.wait_ge(sem.pe, bank + 1)
        return S(g.scalar.activation(T.w[:, at:at + n], T.ps[:, 512 * bank + lo:512 * bank + lo + n], COPY))

    done = []
    for i in range(3):
        o = W * i
        bank = 2 * i + 1
        if i == 0:
            s_z = s_copy(0, o + WZ, ZB - EARLY, 128)
            s_copy(0, o + WP + EARLY - RUN2, 0, ZB - EARLY)
            s_p = s_copy(2, o + WP, 0, EARLY - RUN2)
        else:
            s_z = s_copy(bank + 1, o + WZ, PN, 128)
            s_p = s_copy(bank + 1, o + WP, 0, PN)
        g.vector.wait_ge(sem.pe, bank + 1)
        v_c = V(g.vector.tensor_copy(T.w[:, o:o + RUN1], T.ps[:, 512 * bank:512 * bank + RUN1]))
        g.vector.wait_ge(sem.sa, s_z)
        vw(v_c)
        v_g = V(g.vector.tensor_copy(T.res[:, 512 * i:512 * i + TC], T.w[:, o + XB:o + XB + SLOTS].indirect(T.offs[:, 0:16])))
        g.scalar.wait_ge(sem.sa, s_p)
        g.scalar.wait_ge(sem.v, v_c)
        s_g = S(g.scalar.activation(T.res[:, 512 * i + TC:512 * i + 512], T.w[:, o:o + W].indirect(T.offs[:, 16:32]), COPY))
        done.append((v_g, s_g))
    for i, (dv, ds) in enumerate(done):
        b = (2, 0, 1)[i]
        g.wait_ge(sem.v, dv)
        g.wait_ge(sem.sa, ds)
        g.indirect_dma_start(T.y[:], IndirectOffsetOnAxis(ap=T.idx[:, b:b + 1], axis=0), T.res[:, 512 * i:512 * i + 512], None,
                             bounds_check=TC - 1, oob_is_err=False).then_inc(sem.sc, 16)
    g.wait_ge(sem.out, sent)
    g.wait_ge(sem.sc, 48)
